import numpy as np
import ml_dtypes


def mxq(x, axis, fmt="e4m3"):
    dtype, down = {"e4m3": (ml_dtypes.float8_e4m3fn, 7), "e5m2": (ml_dtypes.float8_e5m2, 14)}[fmt]
    v = np.moveaxis(np.asarray(x, np.float32).astype(ml_dtypes.bfloat16).astype(np.float64), axis, -1)
    blocks = v.reshape(v.shape[:-1] + (-1, 32))
    amax = np.abs(blocks).max(-1, keepdims=True)
    byte = np.maximum(np.where(amax > 0, np.frexp(amax)[1] - 1 + 127, 0) - down, 1)
    scale = np.exp2(byte - 127.0)
    codes = (blocks / scale).astype(np.float32).astype(dtype).astype(np.float64)
    return np.moveaxis((codes * scale).reshape(v.shape), -1, axis)


WIDE = False


def mx_kscale(k):
    if not WIDE:
        return np.ones(k)
    levels = np.array([30, -30])
    if k % 512:
        return np.exp2(np.random.permutation(np.resize(levels, k // 32))).repeat(32)
    a = np.empty((k // 512, 16))
    for p in range(k // 512):
        a[p, :8] = np.random.permutation(np.resize(levels, 8))
        for g in range(8):
            far = levels[np.abs(levels - a[p, g]) >= 10]
            a[p, g + 8] = far[np.random.randint(len(far))]
    return np.exp2(a.ravel()).repeat(32)


def f64(x):
    return np.asarray(x).astype(np.float64)


def striped(idx):
    return np.tile(np.asarray(idx).reshape(-1, 16).T, (8, 1)).astype(np.uint16)


def unstriped(offs):
    return offs[:16].T.reshape(-1).astype(np.int64)


def bf(x):
    return np.asarray(x, np.float32).astype(ml_dtypes.bfloat16)


def planes(Y):
    r, m = Y.shape
    b = f64(bf(Y)).reshape(r // 32, 32, m)
    amax = np.abs(b).max(1)
    byte = np.clip(np.where(amax > 0, np.frexp(amax)[1] - 1 + 127 - 7, 1), 1, 254)
    codes = (b * np.exp2(127.0 - byte)[:, None, :]).reshape(r, m).astype(np.float32).astype(ml_dtypes.float8_e4m3fn).view(np.uint8)
    words = codes.reshape(r // 512, 128, 4, m).transpose(0, 1, 3, 2)
    return np.ascontiguousarray(words), np.ascontiguousarray(byte.astype(np.uint8).reshape(r // 512, 16, m))


K, J, N, T, V = 512, 512, 256, 1024, 1024


def setup_inputs():
    n = np.random.standard_normal
    idx = np.random.permutation(T)[:J]
    idx2 = np.random.permutation(V)[:J]
    fj = mx_kscale(J)
    return {
        "xf": (n((K, T)) * np.random.uniform(0.4, 1.6, (1, T))).astype(np.float32),
        "ca": (np.random.uniform(0.5, 1.5, (J, 1)) * fj[:, None]).astype(np.float32),
        "gt": (n((N, V)) * np.exp(0.5 * n((1, V)))).astype(np.float32),
        "rb": (np.random.uniform(0.5, 1.5, (1, J)) / fj).astype(np.float32),
        "cp": (np.random.uniform(0.4, 1.2, (N, 1))).astype(np.float32),
        "bn": (np.random.uniform(-0.5, 0.5, (1, N))).astype(np.float32),
        "offs": striped(idx),
        "offs2": striped(idx2),
    }


def reference(xf, ca, gt, rb, cp, bn, offs, offs2):
    idx = unstriped(offs)
    idx2 = unstriped(offs2)
    xj = f64(xf)[:, idx].T
    uj = xj / (np.mean(np.abs(xj), axis=1, keepdims=True) + 0.1) * f64(ca)
    gs = np.minimum(f64(gt)[:, idx2], f64(cp)) * f64(rb)
    gj = gs.T
    ujq = mxq(uj, 0, "e5m2")
    gjq = mxq(gj, 0, "e5m2")
    w = ujq.T @ gjq
    ew = np.exp(0.02 * w + f64(bn))
    y = 256.0 * ew / np.sum(ew, axis=1, keepdims=True)
    words, scales = planes(y)
    return y, words, scales

from contextlib import ExitStack

import concourse.mybir as mybir
from concourse.masks import make_identity

K, J, N, T, V = 512, 512, 256, 1024, 1024
FLOPS = 2 * K * J * N

F32 = mybir.dt.float32
BF16 = mybir.dt.bfloat16
I32 = mybir.dt.int32
U32 = mybir.dt.uint32
U16 = mybir.dt.uint16
U8 = mybir.dt.uint8
E5M2X4 = mybir.dt.float8_e5m2_x4
E4M3X4 = mybir.dt.float8_e4m3fn_x4
ALU = mybir.AluOpType
ACT = mybir.ActivationFunctionType
AXIS_X = mybir.AxisListType.X

P = 128
PACK = 4
HALVES = N // P


def tile_list_moment_sized_bounded_shares_pl_kernel(tc, xf, ca, gt, rb, cp, bn, offs, offs2, out_0, out_1, out_2):
    nc = tc.nc
    with ExitStack() as ctx:
        sb = ctx.enter_context(tc.tile_pool(name="sb", bufs=1))
        ps = ctx.enter_context(tc.psum_pool(name="ps", bufs=1))

        x_list = sb.tile([P, J // 16], U16, name="x_list")
        g_list = sb.tile([P, J // 16], U16, name="g_list")
        x_rows = xf.rearrange("(p t) c -> t p c", t=PACK)
        g_rows = gt.rearrange("(p h) v -> h p v", h=HALVES)
        x_win = [sb.tile([P, T], F32, name=f"x_win{t}") for t in range(PACK)]
        g_win = [sb.tile([P, V], F32, name=f"g_win{h}") for h in range(HALVES)]
        nc.sync.dma_start(x_list[:], offs)
        for t in range(PACK):
            nc.sync.dma_start(x_win[t][:], x_rows[t])
        nc.sync.dma_start(g_list[:], offs2)
        for h in range(HALVES):
            nc.sync.dma_start(g_win[h][:], g_rows[h])

        ident = sb.tile([P, P], F32, name="ident")
        make_identity(nc, ident[:])
        rb_col = sb.tile([P, PACK], F32, name="rb_col")
        bn_col = sb.tile([P, 2], F32, name="bn_col")
        ca_col = sb.tile([P, PACK], F32, name="ca_col")
        cp_col = sb.tile([P, HALVES], F32, name="cp_col")
        nc.scalar.dma_start(bn_col[:], bn.rearrange("o (m e) -> (o m) e", e=2))
        nc.scalar.dma_start(rb_col[:], rb.rearrange("o (q i) -> (o q) i", i=PACK))
        nc.scalar.dma_start(ca_col[:], ca.rearrange("(q i) o -> q (i o)", i=PACK))
        nc.scalar.dma_start(cp_col[:], cp.rearrange("(p h) o -> p (h o)", h=HALVES))

        bn_bank = ps.tile([P, 2, P], F32, name="bn_bank", tag="z_bank", bufs=2)
        for e in range(2):
            nc.tensor.transpose(bn_bank[:, e, :], bn_col[:, e : e + 1].to_broadcast([P, P]), ident[:])
        bn_all = sb.tile([P, P, 2], F32, name="bn_all")
        nc.scalar.copy(bn_all[:], bn_bank[:].rearrange("p e m -> p m e"))
        rb_bank = ps.tile([P, PACK, P], F32, name="rb_bank")
        for i in range(PACK):
            nc.tensor.transpose(rb_bank[:, i, :], rb_col[:, i : i + 1].to_broadcast([P, P]), ident[:])

        mean_part = sb.tile([P, PACK, PACK], F32, name="mean_part")
        magnitudes = sb.tile([P, PACK, PACK, P], BF16, name="magnitudes")
        x_bank = []
        for t in range(PACK):
            picked = sb.tile([P, PACK, P], F32, name=f"x_picked{t}")
            nc.vector.tensor_copy(picked[:].rearrange("p i q -> p q i"), x_win[t][:].indirect(x_list[:]))
            bank = ps.tile([P, PACK, P], F32, name=f"x_bank{t}", tag=f"bank{t}")
            for i in range(PACK):
                nc.tensor.transpose(bank[:, i, :], picked[:, i, :], ident[:])
            for i in range(PACK):
                nc.scalar.activation(magnitudes[:, t, i, :], bank[:, i, :], ACT.Abs, scale=1.0 / K,
                                     accum_out=mean_part[:, t, i : i + 1])
            x_bank.append(bank)
            if t == PACK - 2:
                mean_early = sb.tile([P, PACK], F32, name="mean_early")
                nc.vector.tensor_reduce(mean_early[:], mean_part[:, 0 : PACK - 1, :].rearrange("q t i -> q i t"), AXIS_X, ALU.add)

        g_codes = sb.tile([P, N], U32, name="g_codes", align_bytes=64)
        g_scales = sb.tile([P, N], U8, name="g_scales", align_bytes=64)
        g_picked = [sb.tile([P, J], F32, name=f"g_picked{h}") for h in range(HALVES)]

        def bound_and_turn(h):
            rounded = sb.tile([P, P, PACK], BF16, name=f"g_rounded{h}", align_bytes=64)
            nc.vector.scalar_tensor_tensor(rounded[:], g_picked[h][:].rearrange("p (q i) -> p q i", i=PACK),
                                           cp_col[:, h : h + 1], rb_bank[:].rearrange("p i q -> p q i"), ALU.min, ALU.mult)
            words = rounded[:].rearrange("p q i -> p (q i)").bitcast(F32)
            bank = ps.tile([P, 2, P], F32, name=f"g_bank{h}", tag="g_bank")
            for u in range(2):
                nc.tensor.transpose(bank[:, u, :], words[:, u : 2 * P : 2], ident[:])
            grouped = sb.tile([P, P * PACK], BF16, name=f"g_grouped{h}", align_bytes=64)
            nc.scalar.copy(grouped[:].bitcast(F32).rearrange("q (n u) -> q n u", u=2), bank[:].rearrange("q u n -> q n u"))
            return grouped

        def quantise_g(h, grouped):
            cols = slice(h * P, (h + 1) * P)
            nc.vector.quantize_mx(g_codes[:, cols].bitcast(E5M2X4), g_scales[:, cols], grouped[:])

        nc.vector.tensor_copy(g_picked[0][:], g_win[0][:].indirect(g_list[:]))
        nc.scalar.activation(g_picked[1][:], g_win[1][:].indirect(g_list[:]), ACT.Copy)

        denom = sb.tile([P, PACK], F32, name="denom")
        inverse = sb.tile([P, PACK], F32, name="inverse")
        factor = sb.tile([P, PACK], F32, name="factor")
        nc.vector.scalar_tensor_tensor(denom[:], mean_part[:, PACK - 1, :], 0.1, mean_early[:], ALU.add, ALU.add)
        grouped0 = bound_and_turn(0)
        nc.vector.reciprocal(inverse[:], denom[:])
        nc.vector.tensor_tensor(factor[:], inverse[:], ca_col[:], ALU.mult)

        u_rounded = [sb.tile([P, P, PACK], BF16, name=f"u_rounded{t}", align_bytes=64) for t in range(PACK)]
        u_codes = [sb.tile([P, P], U32, name=f"u_codes{t}", align_bytes=64) for t in range(PACK)]
        u_scales = [sb.tile([P, P], U8, name=f"u_scales{t}", align_bytes=64) for t in range(PACK)]

        def scale_u(t):
            nc.vector.tensor_tensor(u_rounded[t][:], x_bank[t][:].rearrange("q i p -> q p i"),
                                    factor[:].unsqueeze(1).to_broadcast([P, P, PACK]), ALU.mult)

        def scale_u_on_scalar(t):
            planes = sb.tile([P, PACK, P], BF16, name="u_planes")
            for i in range(PACK):
                nc.scalar.activation(planes[:, i, :], x_bank[t][:, i, :], ACT.Copy, scale=factor[:, i : i + 1])
            nc.scalar.copy(u_rounded[t][:], planes[:].rearrange("q i p -> q p i"))

        def quantise_u(t):
            nc.vector.quantize_mx(u_codes[t][:].bitcast(E5M2X4), u_scales[t][:], u_rounded[t][:].rearrange("q p i -> q (p i)"))

        scale_u(0)
        grouped1 = bound_and_turn(1)
        quantise_g(0, grouped0)
        quantise_u(0)
        scale_u(1)
        quantise_g(1, grouped1)
        scale_u_on_scalar(3)

        logit = sb.tile([P, PACK, N], F32, name="logit")
        lowest = sb.tile([P, PACK], F32, name="lowest")
        raised = sb.tile([P, PACK, N], F32, name="raised")
        total = sb.tile([P, PACK], F32, name="total")
        share = sb.tile([P, PACK], F32, name="share")
        y = sb.tile([P, PACK, N], F32, name="y")
        y_rows = out_0.rearrange("(p t) n -> t p n", t=PACK)
        w_bank = {}

        def multiply(t):
            w_bank[t] = ps.tile([P, PACK, P], F32, name=f"w_bank{t}", tag=f"bank{t}")
            w = w_bank[t][:].rearrange("p i q -> p (i q)")[:, 0:N]
            nc.tensor.matmul_mx(w, lhsT=u_codes[t][:].bitcast(E5M2X4), lhsT_scale=u_scales[t][:],
                                rhs=g_codes[:].bitcast(E5M2X4), rhs_scale=g_scales[:], start=True, stop=True)
            return w

        def negated_logits(t, w):
            nc.vector.scalar_tensor_tensor(logit[:, t, :].rearrange("p (m h) -> p m h", h=HALVES), w.rearrange("p (h m) -> p m h", h=HALVES),
                                           -0.02, bn_all[:], ALU.mult, ALU.subtract)

        def raise_row(t):
            nc.vector.tensor_reduce(lowest[:, t : t + 1], logit[:, t, :], AXIS_X, ALU.min)
            nc.scalar.activation(raised[:, t, :], logit[:, t, :], ACT.Exp, bias=lowest[:, t : t + 1], scale=-1.0,
                                 accum_out=total[:, t : t + 1])

        logit_n = sb.tile([P, 2, HALVES, P], F32, name="logit_n")
        z_bank = {}

        def multiply_turned(t):
            w_bank[t] = ps.tile([P, PACK, P], F32, name=f"w_bank{t}", tag=f"bank{t}")
            for h in range(HALVES):
                cols = slice(h * P, (h + 1) * P)
                nc.tensor.matmul_mx(w_bank[t][:, h, :], lhsT=g_codes[:, cols].bitcast(E5M2X4), lhsT_scale=g_scales[:, cols],
                                    rhs=u_codes[t][:].bitcast(E5M2X4), rhs_scale=u_scales[t][:], start=True, stop=True)
            for h in range(HALVES):
                nc.scalar.activation(logit_n[:, t, h, :], w_bank[t][:, h, :], ACT.Identity, bias=bn_col[:, h : h + 1], scale=0.02)

        def turn(t):
            z_bank[t] = ps.tile([P, HALVES, P], F32, name=f"z_bank{t}", tag="z_bank", bufs=2)
            for h in range(HALVES):
                nc.tensor.transpose(z_bank[t][:, h, :], logit_n[:, t, h, :], ident[:])

        def raise_turned(t):
            nc.vector.tensor_reduce(lowest[:, t : t + 1], z_bank[t][:].rearrange("p h m -> p (h m)"), AXIS_X, ALU.max, negate=True)
            nc.scalar.activation(raised[:, t, :].rearrange("p (m h) -> p m h", h=HALVES), z_bank[t][:].rearrange("p h m -> p m h"),
                                 ACT.Exp, bias=lowest[:, t : t + 1], accum_out=total[:, t : t + 1])

        def normalise(t):
            nc.vector.reciprocal(share[:, t : t + 1], total[:, t : t + 1])
            nc.vector.tensor_scalar(y[:, t, :], raised[:, t, :], share[:, t : t + 1], 256.0, ALU.mult, ALU.mult)
            nc.sync.dma_start(y_rows[t], y[:, t, :])

        multiply_turned(0)
        quantise_u(1)
        multiply_turned(1)
        scale_u(2)
        turn(0)
        turn(1)
        quantise_u(3)
        quantise_u(2)
        w3 = multiply(3)
        w2 = multiply(2)
        raise_turned(0)
        negated_logits(3, w3)
        raise_turned(1)
        negated_logits(2, w2)
        raise_row(3)
        raise_row(2)
        for t in (0, 1, 3, 2):
            normalise(t)

        y_codes = sb.tile([P, N], U32, name="y_codes", align_bytes=64)
        y_scales = sb.tile([P, N], U8, name="y_scales", align_bytes=64)
        y_rounded = [sb.tile([P, P, PACK], BF16, name=f"y_rounded{c}", align_bytes=64) for c in range(2)]
        nc.scalar.copy(y_rounded[1][:], y[:, :, P:N].rearrange("p t n -> p n t"))
        nc.vector.tensor_copy(y_rounded[0][:], y[:, :, 0:P].rearrange("p t n -> p n t"))
        for c in range(2):
            cols = slice(c * P, (c + 1) * P)
            nc.vector.quantize_mx(y_codes[:, cols].bitcast(E4M3X4), y_scales[:, cols], y_rounded[c][:].rearrange("p n t -> p (n t)"))
        nc.sync.dma_start(out_1.rearrange("z p c r -> (z p) (c r)").bitcast(I32), y_codes[:].bitcast(I32))
        scale_rows = out_2.rearrange("z q c -> (z q) c").bitcast(I32)
        for quad in range(4):
            queue = nc.scalar if quad % 2 == 0 else nc.sync
            queue.dma_start(scale_rows[4 * quad : 4 * quad + 4, :], y_scales[32 * quad : 32 * quad + 4, :].bitcast(I32))
